import numpy as np
import ml_dtypes


def mxq(x, axis, fmt="e4m3"):
    dtype, down = {"e4m3": (ml_dtypes.float8_e4m3fn, 7), "e5m2": (ml_dtypes.float8_e5m2, 14)}[fmt]
    v = np.moveaxis(np.asarray(x, np.float32).astype(ml_dtypes.bfloat16).astype(np.float64), axis, -1)
    blocks = v.reshape(v.shape[:-1] + (-1, 32))
    amax = np.abs(blocks).max(-1, keepdims=True)
    byte = np.maximum(np.where(amax > 0, np.frexp(amax)[1] - 1 + 127, 0) - down, 1)
    scale = np.exp2(byte - 127.0)
    codes = (blocks / scale).astype(np.float32).astype(dtype).astype(np.float64)
    return np.moveaxis((codes * scale).reshape(v.shape), -1, axis)


WIDE = False


def mx_kscale(k):
    if not WIDE:
        return np.ones(k)
    levels = np.array([10, -10, 5, -5, 0])
    if k % 512:
        return np.exp2(np.random.permutation(np.resize(levels, k // 32))).repeat(32)
    a = np.empty((k // 512, 16))
    for p in range(k // 512):
        a[p, :8] = np.random.permutation(np.resize(levels, 8))
        for g in range(8):
            far = levels[np.abs(levels - a[p, g]) >= 10]
            a[p, g + 8] = far[np.random.randint(len(far))]
    return np.exp2(a.ravel()).repeat(32)


def f64(x):
    return np.asarray(x).astype(np.float64)


def striped(idx):
    return np.tile(idx.reshape(-1, 16).T, (8, 1)).astype(np.uint16)


def unstriped(offs):
    return offs[:16].T.reshape(-1).astype(np.int64)


def pack_weight(w):
    k, n = w.shape
    w = f64(np.asarray(w, np.float32).astype(ml_dtypes.bfloat16)).reshape(k // 32, 32, n)
    amax = np.abs(w).max(1)
    byte = np.clip(np.where(amax > 0, np.frexp(amax)[1] - 1 + 127 - 7, 1), 1, 254)
    scaled = (w * np.exp2(127.0 - byte)[:, None, :]).reshape(k, n).astype(np.float32)
    words = np.ascontiguousarray(scaled.reshape(k // 512, 128, 4, n).transpose(0, 1, 3, 2)).astype(ml_dtypes.float8_e4m3fn).view(np.uint8)
    return words, np.ascontiguousarray(byte.astype(np.uint8).reshape(k // 512, 16, n))


def unpack_weight(words, scales):
    g, p, n, _ = words.shape
    vals = np.ascontiguousarray(words).view(ml_dtypes.float8_e4m3fn).astype(np.float64) * np.repeat(np.exp2(scales.astype(np.float64) - 127.0), 8, axis=1)[..., None]
    return vals.transpose(0, 1, 3, 2).reshape(g * 512, n)


def sigmoid(v):
    return 1.0 / (1.0 + np.exp(-np.maximum(v, -700.0)))


K, T, S, H, G, V = 1024, 1024, 512, 512, 1024, 512
P = 2 ** 7


def setup_inputs():
    n = np.random.standard_normal
    s = mx_kscale(K)[:, None]
    u = mx_kscale(H)
    packed_xT = pack_weight(n((K, T)) * s)
    packed_vT = pack_weight(n((H, G)) / np.sqrt(H) / u[:, None])
    packed_gT = pack_weight(n((H, G)) / np.sqrt(H) / u[:, None])
    return {
        "x_words": packed_xT[0],
        "x_scales": packed_xT[1],
        "w1": (n((K, H)) / np.sqrt(K) / s).astype(np.float32),
        "wpos": (np.random.uniform(0.5, 1.5, (H, 1)) * u[:, None]).astype(np.float32),
        "wneg": (np.random.uniform(0.5, 1.5, (H, 1)) * u[:, None]).astype(np.float32),
        "v_words": packed_vT[0],
        "v_scales": packed_vT[1],
        "g_words": packed_gT[0],
        "g_scales": packed_gT[1],
        "prior": (np.tile(0.3 * n(G), (P, 1))).astype(np.float32),
        "offs": striped(np.random.permutation(T)[:S]),
        "cand": striped(np.random.permutation(G)[:V]),
    }


def reference(x_words, x_scales, w1, wpos, wneg, v_words, v_scales, g_words, g_scales, prior, offs, cand):
    xq = unpack_weight(x_words, x_scales)[:, unstriped(offs)]
    p = sigmoid(mxq(f64(w1), 0, "e4m3").T @ xq)
    lp = f64(wpos) * np.log(p + 0.02)
    v_cand = unpack_weight(v_words, v_scales)[:, unstriped(cand)]
    ln = f64(wneg) * np.log(-1.0 * p + 1.02)
    g_cand = unpack_weight(g_words, g_scales)[:, unstriped(cand)]
    return (mxq(lp, 0, "e4m3").T @ v_cand + mxq(ln, 0, "e4m3").T @ g_cand) + f64(prior)[:1][:, unstriped(cand)]

@@ -1,0 +1,195 @@
+from contextlib import ExitStack
+
+import concourse.mybir as mybir
+
+F32 = mybir.dt.float32
+BF16 = mybir.dt.bfloat16
+I32 = mybir.dt.int32
+U32 = mybir.dt.uint32
+U16 = mybir.dt.uint16
+U8 = mybir.dt.uint8
+FP8X4 = mybir.dt.float8_e4m3fn_x4
+ACT = mybir.ActivationFunctionType
+ALU = mybir.AluOpType
+
+P = 128
+PACK = 4
+K, T, S, H, G, V = 1024, 1024, 512, 512, 1024, 512
+FLOPS = 2 * K * H * S + 2 * 2 * H * S * V
+
+
+def tile_picked_ymolrank_score_p_kernel(
+    tc, x_words, x_scales, w1, wpos, wneg, v_words, v_scales, g_words, g_scales, prior, offs, cand, out
+):
+    nc = tc.nc
+    with ExitStack() as ctx:
+        keep = ctx.enter_context(tc.tile_pool(name="keep", bufs=1))
+        psum = ctx.enter_context(tc.psum_pool(name="psum", bufs=1))
+
+        offs_sb = keep.tile([P, S // 16], U16, name="offs_sb")
+        cand_sb = keep.tile([P, V // 16], U16, name="cand_sb")
+        x_tab = [keep.tile([P, T], I32, name=f"x_tab{o}") for o in range(2)]
+        v_tab = keep.tile([P, G], I32, name="v_tab")
+        g_tab = keep.tile([P, G], I32, name="g_tab")
+        xs_tab = keep.tile([P, T], U8, name="xs_tab")
+        vs_tab = keep.tile([P, G], U8, name="vs_tab")
+        gs_tab = keep.tile([P, G], U8, name="gs_tab")
+        prior_tab = keep.tile([P, G], F32, name="prior_tab")
+        w_raw = [[keep.tile([P, PACK, H // 2], F32, name=f"w_raw{o}_{h}") for h in range(2)] for o in range(2)]
+        wt = keep.tile([P, 2, 8], F32, name="wt")
+
+        for tab in (xs_tab, vs_tab, gs_tab):
+            nc.gpsimd.memset(tab[:].bitcast(I32), 0)
+
+        def words(src):
+            return src.rearrange("p n t -> p (n t)").bitcast(I32)
+
+        def load_w(o, h):
+            nc.sync.dma_start(
+                w_raw[o][h][:],
+                w1[512 * o : 512 * (o + 1), 256 * h : 256 * (h + 1)].rearrange("(p j) c -> p j c", j=PACK),
+            )
+
+        def load_scales(queue, tab, src, rows):
+            for q in range(4):
+                queue.dma_start(
+                    tab[32 * q : 32 * q + rows, :].bitcast(I32), src[:, 4 * q : 4 * q + 4, :].bitcast(I32)
+                )
+
+        nc.sync.dma_start(offs_sb[:], offs)
+        load_scales(nc.sync, xs_tab, x_scales, 8)
+        nc.sync.dma_start(x_tab[0][:], words(x_words[0]))
+        load_w(0, 0)
+        nc.sync.dma_start(cand_sb[:], cand)
+        load_scales(nc.sync, vs_tab, v_scales, 4)
+        load_w(0, 1)
+        load_w(1, 0)
+        nc.sync.dma_start(x_tab[1][:], words(x_words[1]))
+        load_w(1, 1)
+        nc.sync.dma_start(v_tab[:], words(v_words[0]))
+        nc.sync.dma_start(g_tab[:], words(g_words[0]))
+        load_scales(nc.sync, gs_tab, g_scales, 4)
+        nc.sync.dma_start(prior_tab[:], prior)
+        nc.sync.dma_start(wt[:, 0, 0:4], wpos.rearrange("(p j) o -> p (j o)", j=PACK))
+        nc.sync.dma_start(wt[:, 1, 0:4], wneg.rearrange("(p j) o -> p (j o)", j=PACK))
+
+        xs_g = keep.tile([P, S], U8, name="xs_g", align_bytes=64)
+        x_g = [keep.tile([P, S], U32, name=f"x_g{o}", align_bytes=64) for o in range(2)]
+        vs_g = keep.tile([P, V], U8, name="vs_g", align_bytes=64)
+        gs_g = keep.tile([P, V], U8, name="gs_g", align_bytes=64)
+        v_g = keep.tile([P, V], U32, name="v_g", align_bytes=64)
+        g_g = keep.tile([P, V], U32, name="g_g", align_bytes=64)
+        prior_g = keep.tile([P, V], F32, name="prior_g")
+        w_bf = [keep.tile([P, PACK, P, PACK], BF16, name=f"w_bf{o}", align_bytes=64) for o in range(2)]
+        w_codes = [keep.tile([P, H], U32, name=f"w_codes{o}", align_bytes=64) for o in range(2)]
+        w_sc = [keep.tile([P, H], U8, name=f"w_sc{o}", align_bytes=64) for o in range(2)]
+        z = [psum.tile([P, S], F32, name=f"z{t}") for t in range(PACK)]
+
+        def deal_w(eng, o, h, m0, m1):
+            src = w_raw[o][h][:, :, 4 * m0 : 4 * m1].rearrange("p j (m t) -> p m j t", t=PACK)
+            dst = w_bf[o][:, :, 64 * h + m0 : 64 * h + m1, :].rearrange("p t m j -> p m j t")
+            if eng == "s":
+                nc.scalar.copy(dst, src)
+            else:
+                nc.vector.tensor_copy(dst, src)
+
+        def quant_w(o, t0, t1):
+            nc.vector.quantize_mx(
+                out=w_codes[o][:, P * t0 : P * t1].bitcast(FP8X4),
+                scales=w_sc[o][:, P * t0 : P * t1],
+                in_=w_bf[o][:, t0:t1, :, :].rearrange("p t m j -> p (t m j)"),
+            )
+
+        def mm1(o, t):
+            nc.tensor.matmul_mx(
+                out=z[t][:],
+                lhsT=w_codes[o][:, P * t : P * (t + 1)].bitcast(FP8X4),
+                lhsT_scale=w_sc[o][:, P * t : P * (t + 1)],
+                rhs=x_g[o][:].bitcast(FP8X4),
+                rhs_scale=xs_g[4 * o : P, :],
+                start=(o == 0),
+                stop=(o == 1),
+            )
+
+        def gather(dst, window, lst):
+            nc.vector.tensor_copy(dst[:], window.indirect(lst[:]))
+
+        deal_w("s", 0, 0, 0, 64)
+        gather(xs_g, xs_tab[:], offs_sb)
+        gather(x_g[0], x_tab[0][:].bitcast(U32), offs_sb)
+        deal_w("s", 0, 1, 0, 64)
+        gather(vs_g, vs_tab[:], cand_sb)
+        quant_w(0, 0, 4)
+        for t in range(PACK):
+            mm1(0, t)
+        deal_w("s", 1, 0, 0, 64)
+        gather(x_g[1], x_tab[1][:].bitcast(U32), offs_sb)
+        deal_w("s", 1, 1, 0, 24)
+        deal_w("v", 1, 1, 24, 64)
+        quant_w(1, 0, 1)
+        quant_w(1, 1, 2)
+        quant_w(1, 2, 4)
+        th = keep.tile([P, PACK, S], F32, name="th")
+        for t in range(PACK):
+            mm1(1, t)
+            nc.scalar.activation(th[:, t, :], z[t][:], ACT.Tanh, scale=0.5)
+        gather(v_g, v_tab[:].bitcast(U32), cand_sb)
+        gather(g_g, g_tab[:].bitcast(U32), cand_sb)
+        gather(gs_g, gs_tab[:], cand_sb)
+        gather(prior_g, prior_tab[:], cand_sb)
+
+        lg = [keep.tile([P, 2, P, PACK], F32, name=f"lg{c}") for c in range(4)]
+        lb = [keep.tile([P, 2, P, PACK], BF16, name=f"lb{c}", align_bytes=64) for c in range(4)]
+        l_codes = [keep.tile([P, 2 * P], U32, name=f"l_codes{c}", align_bytes=64) for c in range(4)]
+        l_sc = [keep.tile([P, 2 * P], U8, name=f"l_sc{c}", align_bytes=64) for c in range(4)]
+        acc = [psum.tile([P, V], F32, name=f"acc{c}") for c in range(4)]
+        res = [keep.tile([P, V], F32, name=f"res{c}") for c in range(4)]
+
+        def logs(c):
+            src = th[:, :, P * c : P * (c + 1)].rearrange("p j (a i) -> p a j i", i=4)
+            for s, sign in enumerate((0.5, -0.5)):
+                dst = lg[c][:, s, :, :].rearrange("p (a i) j -> p a j i", i=4)
+                nc.scalar.activation(dst, src, ACT.Ln, bias=0.52, scale=sign)
+
+        def weigh(c, s):
+            nc.vector.tensor_tensor(
+                lb[c][:, s, :, :], lg[c][:, s, :, :],
+                wt[:, s, 0:4].unsqueeze(1).to_broadcast([P, P, PACK]), ALU.mult,
+            )
+
+        def quant_l(c, s0, s1):
+            nc.vector.quantize_mx(
+                out=l_codes[c][:, P * s0 : P * s1].bitcast(FP8X4), scales=l_sc[c][:, P * s0 : P * s1],
+                in_=lb[c][:, s0:s1, :, :].rearrange("p s t j -> p (s t j)"),
+            )
+            for s in range(s0, s1):
+                codes, sc = ((v_g, vs_g), (g_g, gs_g))[s]
+                nc.tensor.matmul_mx(
+                    out=acc[c][:],
+                    lhsT=l_codes[c][:, P * s : P * (s + 1)].bitcast(FP8X4),
+                    lhsT_scale=l_sc[c][:, P * s : P * (s + 1)],
+                    rhs=codes[:].bitcast(FP8X4),
+                    rhs_scale=sc[:],
+                    start=(s == 0),
+                    stop=(s == 1),
+                )
+
+        def finish(c, v0, v1):
+            nc.vector.tensor_tensor(res[c][:, v0:v1], acc[c][:, v0:v1], prior_g[:, v0:v1], ALU.add)
+            nc.sync.dma_start(out[P * c : P * (c + 1), v0:v1], res[c][:, v0:v1])
+
+        for c in range(4):
+            logs(c)
+        for c in range(4):
+            weigh(c, 0)
+            if c >= 1:
+                quant_l(c - 1, 0, 2)
+            weigh(c, 1)
+            if c == 3:
+                quant_l(c, 0, 1)
+            if c >= 2:
+                finish(c - 2, 0, V)
+        quant_l(3, 1, 2)
+        finish(2, 0, V)
+        finish(3, 0, V // 2)
+        finish(3, V // 2, V)

@@ -1,6 +1,7 @@
 from contextlib import ExitStack
 
 import concourse.mybir as mybir
+from concourse.masks import make_identity
 
 F32 = mybir.dt.float32
 BF16 = mybir.dt.bfloat16
@@ -35,20 +36,27 @@ def tile_picked_ymolrank_score_p_kernel(
         vs_tab = keep.tile([P, G], U8, name="vs_tab")
         gs_tab = keep.tile([P, G], U8, name="gs_tab")
         prior_tab = keep.tile([P, G], F32, name="prior_tab")
-        w_raw = [[keep.tile([P, PACK, H // 2], F32, name=f"w_raw{o}_{h}") for h in range(2)] for o in range(2)]
+        w_raw = {
+            (0, 0): keep.tile([P, PACK, H], F32, name="w_raw0"),
+            (1, 0): keep.tile([P, 2, H], F32, name="w_raw1a"),
+            (1, 2): keep.tile([P, 2, H], F32, name="w_raw1b"),
+        }
         wt = keep.tile([P, 2, 8], F32, name="wt")
 
-        for tab in (xs_tab, vs_tab, gs_tab):
-            nc.gpsimd.memset(tab[:].bitcast(I32), 0)
+        ident = keep.tile([P, P], F32, name="ident")
+        nc.gpsimd.memset(xs_tab[:].bitcast(I32), 0)
+        nc.gpsimd.memset(prior_tab[:], 0.0)
+        nc.gpsimd.memset(vs_tab[:].bitcast(I32), 0)
+        nc.gpsimd.memset(gs_tab[:].bitcast(I32), 0)
+        make_identity(nc, ident[:])
 
         def words(src):
             return src.rearrange("p n t -> p (n t)").bitcast(I32)
 
-        def load_w(o, h):
-            nc.sync.dma_start(
-                w_raw[o][h][:],
-                w1[512 * o : 512 * (o + 1), 256 * h : 256 * (h + 1)].rearrange("(p j) c -> p j c", j=PACK),
-            )
+        def load_w(o, j0):
+            raw = w_raw[(o, j0)]
+            rows = w1[512 * o : 512 * (o + 1), :].rearrange("(p j) c -> p j c", j=PACK)
+            nc.sync.dma_start(raw[:], rows[:, j0 : j0 + raw.shape[1], :])
 
         def load_scales(queue, tab, src, rows):
             for q in range(4):
@@ -58,18 +66,17 @@ def tile_picked_ymolrank_score_p_kernel(
 
         nc.sync.dma_start(offs_sb[:], offs)
         load_scales(nc.sync, xs_tab, x_scales, 8)
-        nc.sync.dma_start(x_tab[0][:], words(x_words[0]))
         load_w(0, 0)
         nc.sync.dma_start(cand_sb[:], cand)
-        load_scales(nc.sync, vs_tab, v_scales, 4)
-        load_w(0, 1)
+        nc.sync.dma_start(prior_tab[0:1, :], prior[0:1, :])
+        nc.sync.dma_start(x_tab[0][:], words(x_words[0]))
         load_w(1, 0)
         nc.sync.dma_start(x_tab[1][:], words(x_words[1]))
-        load_w(1, 1)
+        load_w(1, 2)
+        load_scales(nc.sync, vs_tab, v_scales, 4)
         nc.sync.dma_start(v_tab[:], words(v_words[0]))
         nc.sync.dma_start(g_tab[:], words(g_words[0]))
         load_scales(nc.sync, gs_tab, g_scales, 4)
-        nc.sync.dma_start(prior_tab[:], prior)
         nc.sync.dma_start(wt[:, 0, 0:4], wpos.rearrange("(p j) o -> p (j o)", j=PACK))
         nc.sync.dma_start(wt[:, 1, 0:4], wneg.rearrange("(p j) o -> p (j o)", j=PACK))
 
@@ -79,15 +86,19 @@ def tile_picked_ymolrank_score_p_kernel(
         gs_g = keep.tile([P, V], U8, name="gs_g", align_bytes=64)
         v_g = keep.tile([P, V], U32, name="v_g", align_bytes=64)
         g_g = keep.tile([P, V], U32, name="g_g", align_bytes=64)
+        prior_row = keep.tile([P, V], F32, name="prior_row")
+        prior_col = keep.tile([P, PACK], F32, name="prior_col")
         prior_g = keep.tile([P, V], F32, name="prior_g")
-        w_bf = [keep.tile([P, PACK, P, PACK], BF16, name=f"w_bf{o}", align_bytes=64) for o in range(2)]
+        acc = [psum.tile([P, V], F32, name=f"acc{c}") for c in range(4)]
+        w_bf = [keep.tile([P, PACK, P, PACK], BF16, name=f"w_bf{o}", tag=f"w_bf{o}", align_bytes=64) for o in range(2)]
         w_codes = [keep.tile([P, H], U32, name=f"w_codes{o}", align_bytes=64) for o in range(2)]
         w_sc = [keep.tile([P, H], U8, name=f"w_sc{o}", align_bytes=64) for o in range(2)]
         z = [psum.tile([P, S], F32, name=f"z{t}") for t in range(PACK)]
 
-        def deal_w(eng, o, h, m0, m1):
-            src = w_raw[o][h][:, :, 4 * m0 : 4 * m1].rearrange("p j (m t) -> p m j t", t=PACK)
-            dst = w_bf[o][:, :, 64 * h + m0 : 64 * h + m1, :].rearrange("p t m j -> p m j t")
+        def deal_w(eng, o, j0, t0, t1):
+            raw = w_raw[(o, j0)]
+            src = raw[:].rearrange("p j (m t) -> p m j t", t=PACK)[:, :, :, t0:t1]
+            dst = w_bf[o][:, t0:t1, :, j0 : j0 + raw.shape[1]].rearrange("p t m j -> p m j t")
             if eng == "s":
                 nc.scalar.copy(dst, src)
             else:
@@ -114,18 +125,23 @@ def tile_picked_ymolrank_score_p_kernel(
         def gather(dst, window, lst):
             nc.vector.tensor_copy(dst[:], window.indirect(lst[:]))
 
-        deal_w("s", 0, 0, 0, 64)
         gather(xs_g, xs_tab[:], offs_sb)
+        deal_w("s", 0, 0, 0, 4)
+        gather(prior_row, prior_tab[:], cand_sb)
+        for b in range(4):
+            nc.tensor.transpose(acc[3][:, P * b : P * (b + 1)], prior_row[:, P * b : P * (b + 1)], ident[:])
+        nc.scalar.copy(prior_col[:], acc[3][:, 0:V:P])
+        for b in range(4):
+            nc.tensor.transpose(acc[2][:, P * b : P * (b + 1)], prior_col[:, b : b + 1].to_broadcast([P, P]), ident[:])
+        nc.scalar.copy(prior_g[:], acc[2][:])
         gather(x_g[0], x_tab[0][:].bitcast(U32), offs_sb)
-        deal_w("s", 0, 1, 0, 64)
-        gather(vs_g, vs_tab[:], cand_sb)
         quant_w(0, 0, 4)
         for t in range(PACK):
             mm1(0, t)
-        deal_w("s", 1, 0, 0, 64)
+        deal_w("s", 1, 0, 0, 4)
         gather(x_g[1], x_tab[1][:].bitcast(U32), offs_sb)
-        deal_w("s", 1, 1, 0, 24)
-        deal_w("v", 1, 1, 24, 64)
+        deal_w("v", 1, 2, 0, 2)
+        deal_w("s", 1, 2, 2, 4)
         quant_w(1, 0, 1)
         quant_w(1, 1, 2)
         quant_w(1, 2, 4)
@@ -133,16 +149,15 @@ def tile_picked_ymolrank_score_p_kernel(
         for t in range(PACK):
             mm1(1, t)
             nc.scalar.activation(th[:, t, :], z[t][:], ACT.Tanh, scale=0.5)
+        gather(vs_g, vs_tab[:], cand_sb)
         gather(v_g, v_tab[:].bitcast(U32), cand_sb)
         gather(g_g, g_tab[:].bitcast(U32), cand_sb)
         gather(gs_g, gs_tab[:], cand_sb)
-        gather(prior_g, prior_tab[:], cand_sb)
 
         lg = [keep.tile([P, 2, P, PACK], F32, name=f"lg{c}") for c in range(4)]
         lb = [keep.tile([P, 2, P, PACK], BF16, name=f"lb{c}", align_bytes=64) for c in range(4)]
         l_codes = [keep.tile([P, 2 * P], U32, name=f"l_codes{c}", align_bytes=64) for c in range(4)]
         l_sc = [keep.tile([P, 2 * P], U8, name=f"l_sc{c}", align_bytes=64) for c in range(4)]
-        acc = [psum.tile([P, V], F32, name=f"acc{c}") for c in range(4)]
         res = [keep.tile([P, V], F32, name=f"res{c}") for c in range(4)]
 
         def logs(c):
@@ -185,11 +200,11 @@ def tile_picked_ymolrank_score_p_kernel(
             if c >= 1:
                 quant_l(c - 1, 0, 2)
             weigh(c, 1)
-            if c == 3:
-                quant_l(c, 0, 1)
-            if c >= 2:
-                finish(c - 2, 0, V)
+            if c == 2:
+                finish(0, 0, V)
+        quant_l(3, 0, 1)
         quant_l(3, 1, 2)
+        finish(1, 0, V)
         finish(2, 0, V)
         finish(3, 0, V // 2)
         finish(3, V // 2, V)

from contextlib import ExitStack

import concourse.mybir as mybir
from concourse.masks import make_identity

F32 = mybir.dt.float32
BF16 = mybir.dt.bfloat16
I32 = mybir.dt.int32
U32 = mybir.dt.uint32
U16 = mybir.dt.uint16
U8 = mybir.dt.uint8
FP8X4 = mybir.dt.float8_e4m3fn_x4
ACT = mybir.ActivationFunctionType
ALU = mybir.AluOpType

P = 128
PACK = 4
K, T, S, H, G, V = 1024, 1024, 512, 512, 1024, 512
FLOPS = 2 * K * H * S + 2 * 2 * H * S * V


def tile_picked_ymolrank_score_p_kernel(
    tc, x_words, x_scales, w1, wpos, wneg, v_words, v_scales, g_words, g_scales, prior, offs, cand, out
):
    nc = tc.nc
    with ExitStack() as ctx:
        keep = ctx.enter_context(tc.tile_pool(name="keep", bufs=1))
        psum = ctx.enter_context(tc.psum_pool(name="psum", bufs=1))

        offs_sb = keep.tile([P, S // 16], U16, name="offs_sb")
        cand_sb = keep.tile([P, V // 16], U16, name="cand_sb")
        x_tab = [keep.tile([P, T], I32, name=f"x_tab{o}") for o in range(2)]
        v_tab = keep.tile([P, G], I32, name="v_tab")
        g_tab = keep.tile([P, G], I32, name="g_tab")
        xs_tab = keep.tile([P, T], U8, name="xs_tab")
        vs_tab = keep.tile([P, G], U8, name="vs_tab")
        gs_tab = keep.tile([P, G], U8, name="gs_tab")
        prior_tab = keep.tile([P, G], F32, name="prior_tab")
        w_raw = {
            (0, 0): keep.tile([P, PACK, H], F32, name="w_raw0"),
            (1, 0): keep.tile([P, 2, H], F32, name="w_raw1a"),
            (1, 2): keep.tile([P, 2, H], F32, name="w_raw1b"),
        }
        wt = keep.tile([P, 2, 8], F32, name="wt")

        ident = keep.tile([P, P], F32, name="ident")
        nc.gpsimd.memset(xs_tab[:].bitcast(I32), 0)
        nc.gpsimd.memset(prior_tab[:], 0.0)
        nc.gpsimd.memset(vs_tab[:].bitcast(I32), 0)
        nc.gpsimd.memset(gs_tab[:].bitcast(I32), 0)
        make_identity(nc, ident[:])

        def words(src):
            return src.rearrange("p n t -> p (n t)").bitcast(I32)

        def load_w(o, j0):
            raw = w_raw[(o, j0)]
            rows = w1[512 * o : 512 * (o + 1), :].rearrange("(p j) c -> p j c", j=PACK)
            nc.sync.dma_start(raw[:], rows[:, j0 : j0 + raw.shape[1], :])

        def load_scales(queue, tab, src, rows):
            for q in range(4):
                queue.dma_start(
                    tab[32 * q : 32 * q + rows, :].bitcast(I32), src[:, 4 * q : 4 * q + 4, :].bitcast(I32)
                )

        nc.sync.dma_start(offs_sb[:], offs)
        load_scales(nc.sync, xs_tab, x_scales, 8)
        load_w(0, 0)
        nc.sync.dma_start(cand_sb[:], cand)
        nc.sync.dma_start(prior_tab[0:1, :], prior[0:1, :])
        nc.sync.dma_start(x_tab[0][:], words(x_words[0]))
        load_w(1, 0)
        nc.sync.dma_start(x_tab[1][:], words(x_words[1]))
        load_w(1, 2)
        load_scales(nc.sync, vs_tab, v_scales, 4)
        nc.sync.dma_start(v_tab[:], words(v_words[0]))
        nc.sync.dma_start(g_tab[:], words(g_words[0]))
        load_scales(nc.sync, gs_tab, g_scales, 4)
        nc.sync.dma_start(wt[:, 0, 0:4], wpos.rearrange("(p j) o -> p (j o)", j=PACK))
        nc.sync.dma_start(wt[:, 1, 0:4], wneg.rearrange("(p j) o -> p (j o)", j=PACK))

        xs_g = keep.tile([P, S], U8, name="xs_g", align_bytes=64)
        x_g = [keep.tile([P, S], U32, name=f"x_g{o}", align_bytes=64) for o in range(2)]
        vs_g = keep.tile([P, V], U8, name="vs_g", align_bytes=64)
        gs_g = keep.tile([P, V], U8, name="gs_g", align_bytes=64)
        v_g = keep.tile([P, V], U32, name="v_g", align_bytes=64)
        g_g = keep.tile([P, V], U32, name="g_g", align_bytes=64)
        prior_row = keep.tile([P, V], F32, name="prior_row")
        prior_col = keep.tile([P, PACK], F32, name="prior_col")
        prior_g = keep.tile([P, V], F32, name="prior_g")
        acc = [psum.tile([P, V], F32, name=f"acc{c}") for c in range(4)]
        w_bf = [keep.tile([P, PACK, P, PACK], BF16, name=f"w_bf{o}", tag=f"w_bf{o}", align_bytes=64) for o in range(2)]
        w_codes = [keep.tile([P, H], U32, name=f"w_codes{o}", align_bytes=64) for o in range(2)]
        w_sc = [keep.tile([P, H], U8, name=f"w_sc{o}", align_bytes=64) for o in range(2)]
        z = [psum.tile([P, S], F32, name=f"z{t}") for t in range(PACK)]

        def deal_w(eng, o, j0, t0, t1):
            raw = w_raw[(o, j0)]
            src = raw[:].rearrange("p j (m t) -> p m j t", t=PACK)[:, :, :, t0:t1]
            dst = w_bf[o][:, t0:t1, :, j0 : j0 + raw.shape[1]].rearrange("p t m j -> p m j t")
            if eng == "s":
                nc.scalar.copy(dst, src)
            else:
                nc.vector.tensor_copy(dst, src)

        def quant_w(o, t0, t1):
            nc.vector.quantize_mx(
                out=w_codes[o][:, P * t0 : P * t1].bitcast(FP8X4),
                scales=w_sc[o][:, P * t0 : P * t1],
                in_=w_bf[o][:, t0:t1, :, :].rearrange("p t m j -> p (t m j)"),
            )

        def mm1(o, t):
            nc.tensor.matmul_mx(
                out=z[t][:],
                lhsT=w_codes[o][:, P * t : P * (t + 1)].bitcast(FP8X4),
                lhsT_scale=w_sc[o][:, P * t : P * (t + 1)],
                rhs=x_g[o][:].bitcast(FP8X4),
                rhs_scale=xs_g[4 * o : P, :],
                start=(o == 0),
                stop=(o == 1),
            )

        def gather(dst, window, lst):
            nc.vector.tensor_copy(dst[:], window.indirect(lst[:]))

        gather(xs_g, xs_tab[:], offs_sb)
        deal_w("s", 0, 0, 0, 4)
        gather(prior_row, prior_tab[:], cand_sb)
        for b in range(4):
            nc.tensor.transpose(acc[3][:, P * b : P * (b + 1)], prior_row[:, P * b : P * (b + 1)], ident[:])
        nc.scalar.copy(prior_col[:], acc[3][:, 0:V:P])
        for b in range(4):
            nc.tensor.transpose(acc[2][:, P * b : P * (b + 1)], prior_col[:, b : b + 1].to_broadcast([P, P]), ident[:])
        nc.scalar.copy(prior_g[:], acc[2][:])
        gather(x_g[0], x_tab[0][:].bitcast(U32), offs_sb)
        quant_w(0, 0, 4)
        for t in range(PACK):
            mm1(0, t)
        deal_w("s", 1, 0, 0, 4)
        gather(x_g[1], x_tab[1][:].bitcast(U32), offs_sb)
        deal_w("v", 1, 2, 0, 2)
        deal_w("s", 1, 2, 2, 4)
        quant_w(1, 0, 1)
        quant_w(1, 1, 2)
        quant_w(1, 2, 4)
        th = keep.tile([P, PACK, S], F32, name="th")
        for t in range(PACK):
            mm1(1, t)
            nc.scalar.activation(th[:, t, :], z[t][:], ACT.Tanh, scale=0.5)
        gather(vs_g, vs_tab[:], cand_sb)
        gather(v_g, v_tab[:].bitcast(U32), cand_sb)
        gather(g_g, g_tab[:].bitcast(U32), cand_sb)
        gather(gs_g, gs_tab[:], cand_sb)

        lg = [keep.tile([P, 2, P, PACK], F32, name=f"lg{c}") for c in range(4)]
        lb = [keep.tile([P, 2, P, PACK], BF16, name=f"lb{c}", align_bytes=64) for c in range(4)]
        l_codes = [keep.tile([P, 2 * P], U32, name=f"l_codes{c}", align_bytes=64) for c in range(4)]
        l_sc = [keep.tile([P, 2 * P], U8, name=f"l_sc{c}", align_bytes=64) for c in range(4)]
        res = [keep.tile([P, V], F32, name=f"res{c}") for c in range(4)]

        def logs(c):
            src = th[:, :, P * c : P * (c + 1)].rearrange("p j (a i) -> p a j i", i=4)
            for s, sign in enumerate((0.5, -0.5)):
                dst = lg[c][:, s, :, :].rearrange("p (a i) j -> p a j i", i=4)
                nc.scalar.activation(dst, src, ACT.Ln, bias=0.52, scale=sign)

        def weigh(c, s):
            nc.vector.tensor_tensor(
                lb[c][:, s, :, :], lg[c][:, s, :, :],
                wt[:, s, 0:4].unsqueeze(1).to_broadcast([P, P, PACK]), ALU.mult,
            )

        def quant_l(c, s0, s1):
            nc.vector.quantize_mx(
                out=l_codes[c][:, P * s0 : P * s1].bitcast(FP8X4), scales=l_sc[c][:, P * s0 : P * s1],
                in_=lb[c][:, s0:s1, :, :].rearrange("p s t j -> p (s t j)"),
            )
            for s in range(s0, s1):
                codes, sc = ((v_g, vs_g), (g_g, gs_g))[s]
                nc.tensor.matmul_mx(
                    out=acc[c][:],
                    lhsT=l_codes[c][:, P * s : P * (s + 1)].bitcast(FP8X4),
                    lhsT_scale=l_sc[c][:, P * s : P * (s + 1)],
                    rhs=codes[:].bitcast(FP8X4),
                    rhs_scale=sc[:],
                    start=(s == 0),
                    stop=(s == 1),
                )

        def finish(c, v0, v1):
            nc.vector.tensor_tensor(res[c][:, v0:v1], acc[c][:, v0:v1], prior_g[:, v0:v1], ALU.add)
            nc.sync.dma_start(out[P * c : P * (c + 1), v0:v1], res[c][:, v0:v1])

        for c in range(4):
            logs(c)
        for c in range(4):
            weigh(c, 0)
            if c >= 1:
                quant_l(c - 1, 0, 2)
            weigh(c, 1)
            if c == 2:
                finish(0, 0, V)
        quant_l(3, 0, 1)
        quant_l(3, 1, 2)
        finish(1, 0, V)
        finish(2, 0, V)
        finish(3, 0, V // 2)
        finish(3, V // 2, V)
